import numpy as np
import ml_dtypes


def mxq(x, axis, fmt="e4m3"):
    dtype, down = {"e4m3": (ml_dtypes.float8_e4m3fn, 7), "e5m2": (ml_dtypes.float8_e5m2, 14)}[fmt]
    v = np.moveaxis(np.asarray(x, np.float32).astype(ml_dtypes.bfloat16).astype(np.float64), axis, -1)
    blocks = v.reshape(v.shape[:-1] + (-1, 32))
    amax = np.abs(blocks).max(-1, keepdims=True)
    byte = np.maximum(np.where(amax > 0, np.frexp(amax)[1] - 1 + 127, 0) - down, 1)
    scale = np.exp2(byte - 127.0)
    codes = (blocks / scale).astype(np.float32).astype(dtype).astype(np.float64)
    return np.moveaxis((codes * scale).reshape(v.shape), -1, axis)


WIDE = False


def mx_kscale(k):
    if not WIDE:
        return np.ones(k)
    levels = np.array([10, -10, 5, -5, 0])
    if k % 512:
        return np.exp2(np.random.permutation(np.resize(levels, k // 32))).repeat(32)
    a = np.empty((k // 512, 16))
    for p in range(k // 512):
        a[p, :8] = np.random.permutation(np.resize(levels, 8))
        for g in range(8):
            far = levels[np.abs(levels - a[p, g]) >= 10]
            a[p, g + 8] = far[np.random.randint(len(far))]
    return np.exp2(a.ravel()).repeat(32)


def f64(x):
    return np.asarray(x).astype(np.float64)


def striped(idx):
    return np.tile(idx.reshape(-1, 16).T, (8, 1)).astype(np.uint16)


def unstriped(offs):
    return offs[:16].T.reshape(-1).astype(np.int64)


E2M1 = np.array([0.0, 0.5, 1.0, 1.5, 2.0, 3.0, 4.0, 6.0, -0.0, -0.5, -1.0, -1.5, -2.0, -3.0, -4.0, -6.0])


def pack_weight(w, fmt):
    k, n = w.shape
    w = f64(np.asarray(w, np.float32).astype(ml_dtypes.bfloat16)).reshape(k // 32, 32, n)
    amax = np.abs(w).max(1)
    if fmt == "e4m3":
        byte = np.frexp(amax)[1] - 1 + 127 - 7
    else:
        mant, ex = np.frexp(amax / 6.0)
        byte = np.where(mant > 0.5, ex, ex - 1) + 127
    byte = np.clip(np.where(amax > 0, byte, 1), 1, 254)
    scaled = (w * np.exp2(127.0 - byte)[:, None, :]).reshape(k, n).astype(np.float32)
    by_word = np.ascontiguousarray(scaled.reshape(k // 512, 128, 4, n).transpose(0, 1, 3, 2))
    if fmt == "e4m3":
        words = by_word.astype(ml_dtypes.float8_e4m3fn).view(np.uint8)
    else:
        c = by_word.astype(ml_dtypes.float4_e2m1fn).view(np.uint8) & 0xF
        words = (c[..., 0::2] | (c[..., 1::2] << 4)).reshape(k // 512, 128, 2 * n)
    return np.ascontiguousarray(words), np.ascontiguousarray(byte.astype(np.uint8).reshape(k // 512, 16, n))


def unpack_weight(words, scales, fmt):
    g, _, n = scales.shape
    words = np.ascontiguousarray(words).reshape(g, 128, n, -1)
    if fmt == "e4m3":
        vals = words.view(ml_dtypes.float8_e4m3fn).astype(np.float64)
    else:
        nib = np.empty((g, 128, n, 4), np.uint8)
        nib[..., 0::2] = words & 0xF
        nib[..., 1::2] = words >> 4
        vals = E2M1[nib]
    vals = vals * np.repeat(np.exp2(scales.astype(np.float64) - 127.0), 8, axis=1)[..., None]
    return vals.transpose(0, 1, 3, 2).reshape(g * 512, n)


def gelu(v):
    return 0.5 * v * (1.0 + np.tanh(np.sqrt(2.0 / np.pi) * (v + 0.044715 * v**3)))


K, K2, T, S, H, N = 1024, 512, 4096, 1024, 1024, 512

def setup_inputs():
    n = np.random.standard_normal
    s = mx_kscale(K)[:, None]
    s2 = mx_kscale(K2)[:, None]
    u = mx_kscale(H)[:, None]
    d = {}
    d["tab_words"], d["tab_scales"] = pack_weight(n((K, T)) * s, "e4m3")
    d["offs"] = striped(np.random.permutation(T)[:S])
    d["xs_words"], d["xs_scales"] = pack_weight(n((K2, S)) * s2, "e4m3")
    d["w1"] = (n((K, H)) / K ** 0.5 / s * u.T).astype(np.float32)
    d["w2_words"], d["w2_scales"] = pack_weight(n((K2, H)) / K2 ** 0.5 / s2 * u.T, "e2m1")
    d["leak"] = (n((H, S)) * u).astype(np.float32)
    d["w3"] = (n((H, N)) / H ** 0.5 / u).astype(np.float32)
    d["gain"] = np.exp(0.3 * n(N)).astype(np.float32)
    return d

def reference(tab_words, tab_scales, offs, xs_words, xs_scales, w1, w2_words, w2_scales, leak, w3, gain):
    v = unpack_weight(tab_words, tab_scales, "e4m3")[:, unstriped(offs)]
    xs = unpack_weight(xs_words, xs_scales, "e4m3")
    w2 = unpack_weight(w2_words, w2_scales, "e2m1")
    a = mxq(f64(w1), 0, "e4m3").T @ v
    b = np.abs((w2.T @ xs) + f64(leak))
    z = a - b
    y = mxq(f64(w3), 0, "e4m3").T @ mxq(z, 0, "e4m3")
    return f64(gain)[:, None] * y

@@ -1,0 +1,240 @@
+from contextlib import ExitStack
+
+import concourse.mybir as mybir
+
+K, K2, T, S, H, N = 1024, 512, 4096, 1024, 1024, 512
+FLOPS = 2 * (K * H * S + K2 * H * S + H * N * S)
+
+F32 = mybir.dt.float32
+BF16 = mybir.dt.bfloat16
+I32 = mybir.dt.int32
+U32 = mybir.dt.uint32
+U16 = mybir.dt.uint16
+U8 = mybir.dt.uint8
+FP8X4 = mybir.dt.float8_e4m3fn_x4
+FP4X4 = mybir.dt.float4_e2m1fn_x4
+ADD = mybir.AluOpType.add
+SUB = mybir.AluOpType.subtract
+MULT = mybir.AluOpType.mult
+ABS = mybir.ActivationFunctionType.Abs
+COPY = mybir.ActivationFunctionType.Copy
+
+P = 128
+PACK = 4
+KP = P * PACK
+HALF = 512
+QUARTER = 256
+SLICE = 128
+
+
+def tile_list_lock_flight_features_kernel(
+    tc, tab_words, tab_scales, offs, xs_words, xs_scales, w1, w2_words, w2_scales, leak, w3, gain, out
+):
+    nc = tc.nc
+    with ExitStack() as ctx:
+        held = ctx.enter_context(tc.tile_pool(name="held", bufs=1))
+        stage = ctx.enter_context(tc.tile_pool(name="stage", bufs=8))
+        rounded = ctx.enter_context(tc.tile_pool(name="rounded", bufs=3))
+        psum = ctx.enter_context(tc.psum_pool(name="psum", bufs=4))
+
+        offsets = held.tile([P, S // 16], U16, name="offsets")
+        w2_raw = held.tile([P, 2 * H], U8, name="w2_raw", align_bytes=64)
+        w2_raw_scales = held.tile([P, H], U8, name="w2_raw_scales", align_bytes=64)
+        xs_codes = held.tile([P, S], U32, name="xs_codes", align_bytes=64)
+        xs_plane = held.tile([P, S], U8, name="xs_plane", align_bytes=64)
+        tab_plane = held.tile([P, T], U8, name="tab_plane", align_bytes=64)
+        gains = held.tile([P, PACK], F32, name="gains")
+
+        nc.vector.memset(w2_raw_scales[:].bitcast(I32), 0)
+        nc.vector.memset(xs_plane[:].bitcast(I32), 0)
+        nc.vector.memset(tab_plane[:].bitcast(I32), 0)
+
+        nc.sync.dma_start(out=w2_raw[:].bitcast(I32), in_=w2_words[0].bitcast(I32))
+        nc.sync.dma_start(out=xs_codes[:].bitcast(I32), in_=xs_words[0].rearrange("p c i -> p (c i)").bitcast(I32))
+        for q in range(4):
+            nc.scalar.dma_start(
+                out=w2_raw_scales[32 * q : 32 * q + 4, :].bitcast(I32), in_=w2_scales[0, 4 * q : 4 * q + 4, :].bitcast(I32)
+            )
+        for q in range(4):
+            nc.scalar.dma_start(
+                out=xs_plane[32 * q : 32 * q + 4, :].bitcast(I32), in_=xs_scales[0, 4 * q : 4 * q + 4, :].bitcast(I32)
+            )
+        for q in range(4):
+            nc.scalar.dma_start(
+                out=tab_plane[32 * q : 32 * q + 8, :].bitcast(I32), in_=tab_scales[:, 4 * q : 4 * q + 4, :].bitcast(I32)
+            )
+        nc.scalar.dma_start(out=gains[:], in_=gain.rearrange("(p u) -> p u", u=PACK))
+
+        def load_rows(src, row0, col0, width, name):
+            raw = stage.tile([P, PACK, width], F32, name=name, tag="raw")
+            nc.sync.dma_start(
+                out=raw[:], in_=src[row0 : row0 + KP, col0 : col0 + width].rearrange("(p j) c -> p j c", j=PACK)
+            )
+            return raw
+
+        leak_raw = {}
+        for b in range(2):
+            for h in range(2):
+                leak_raw[b, h] = load_rows(leak, KP * b, HALF * h, HALF, "leak_%d_%d" % (b, h))
+        nc.sync.dma_start(offsets[:], offs)
+
+        def load_table(a):
+            words = held.tile([P, T], U32, name="table_%d" % a, align_bytes=64)
+            nc.sync.dma_start(out=words[:].bitcast(I32), in_=tab_words[a].rearrange("p t i -> p (t i)").bitcast(I32))
+            return words
+
+        table = [load_table(0)]
+        w1_raw = {(0, 0): [load_rows(w1, 0, 0, KP, "w1_0_0")]}
+        table.append(load_table(1))
+        w1_raw[0, 1] = [load_rows(w1, KP, c0, KP // 2, "w1_0_1_%d" % c0) for c0 in (0, KP // 2)]
+        for a in range(2):
+            w1_raw[1, a] = [load_rows(w1, KP * a, KP, KP, "w1_1_%d" % a)]
+        w3_raw = [[load_rows(w3, KP * b, 0, N, "w3_%d" % b)] for b in range(2)]
+
+        w2_codes, w2_plane = [], []
+        for b in range(2):
+            codes = held.tile([P, 2 * KP], U8, name="w2_codes_%d" % b, align_bytes=64)
+            plane = held.tile([P, KP], U8, name="w2_plane_%d" % b, align_bytes=64)
+            nc.vector.tensor_copy(
+                out=codes[:].rearrange("p (t m e) -> p t m e", t=PACK, e=2),
+                in_=w2_raw[:, 2 * KP * b : 2 * KP * (b + 1)].rearrange("p (m t e) -> p t m e", t=PACK, e=2),
+            )
+            nc.vector.tensor_copy(
+                out=plane[:].rearrange("p (t m) -> p t m", t=PACK),
+                in_=w2_raw_scales[:, KP * b : KP * (b + 1)].rearrange("p (m t) -> p t m", t=PACK),
+            )
+            w2_codes.append(codes)
+            w2_plane.append(plane)
+
+        size = {}
+        for b in range(2):
+            for h in range(2):
+                shifted = leak_raw[b, h]
+                for t in range(PACK):
+                    bank = psum.tile([P, HALF], F32, name="c_bank", tag="ab"[t % 2])
+                    nc.tensor.matmul_mx(
+                        out=bank[:],
+                        lhsT=w2_codes[b][:, 2 * P * t : 2 * P * (t + 1)].bitcast(FP4X4),
+                        lhsT_scale=w2_plane[b][:, P * t : P * (t + 1)],
+                        rhs=xs_codes[:, HALF * h : HALF * (h + 1)].bitcast(FP8X4),
+                        rhs_scale=xs_plane[:, HALF * h : HALF * (h + 1)],
+                        start=True,
+                        stop=True,
+                    )
+                    nc.vector.tensor_tensor(out=shifted[:, t, :], in0=bank[:], in1=shifted[:, t, :], op=ADD)
+                size[b, h] = held.tile([P, HALF * PACK], F32, name="size_%d_%d" % (b, h))
+                nc.scalar.activation(
+                    out=size[b, h][:].rearrange("p (c i t) -> p c t i", i=4, t=PACK),
+                    in_=shifted[:].rearrange("p t (c i) -> p c t i", i=4),
+                    func=ABS,
+                )
+
+        picked_plane = held.tile([P, S], U8, name="picked_plane", align_bytes=64)
+        nc.vector.tensor_copy(picked_plane[:], tab_plane[:].indirect(offsets[:]))
+        picked = []
+        for a in range(2):
+            words = held.tile([P, S], U32, name="picked_%d" % a, align_bytes=64)
+            nc.vector.tensor_copy(words[:], table[a][:].indirect(offsets[:]))
+            picked.append(words)
+
+        def quantise_weight(raws, copies, name):
+            grouped = rounded.tile([P, KP * PACK], BF16, name="grouped", align_bytes=64)
+            dealt = grouped[:].rearrange("p (t m j) -> p m j t", t=PACK, j=PACK)
+            step = P // len(raws)
+            for i, (raw, copy) in enumerate(zip(raws, copies)):
+                copy(out=dealt[:, step * i : step * (i + 1)], in_=raw[:].rearrange("p j (m t) -> p m j t", t=PACK))
+            codes = held.tile([P, KP], U32, name=name + "_codes", align_bytes=64)
+            plane = held.tile([P, KP], U8, name=name + "_plane", align_bytes=64)
+            nc.vector.quantize_mx(out=codes[:].bitcast(FP8X4), scales=plane[:], in_=grouped[:])
+            return codes, plane
+
+        w1_mx = {}
+        for b in range(2):
+            for a in range(2):
+                copies = [nc.scalar.copy, nc.vector.tensor_copy] if len(w1_raw[b, a]) == 2 else [nc.scalar.copy]
+                w1_mx[b, a] = quantise_weight(w1_raw[b, a], copies, "w1_%d_%d" % (b, a))
+        w3_mx = [quantise_weight(w3_raw[b], [nc.scalar.copy], "w3_%d" % b) for b in range(2)]
+
+        def chamber_pass(bank, b, s, a):
+            codes, plane = w1_mx[b, a]
+            cols = slice(SLICE * s, SLICE * (s + 1))
+            for t in range(PACK):
+                nc.tensor.matmul_mx(
+                    out=bank[:, t, :],
+                    lhsT=codes[:, P * t : P * (t + 1)].bitcast(FP8X4),
+                    lhsT_scale=plane[:, P * t : P * (t + 1)],
+                    rhs=picked[a][:, cols].bitcast(FP8X4),
+                    rhs_scale=picked_plane[4 * a : P, cols],
+                    start=(a == 0 and t == 0),
+                    stop=(a == 1 and t == PACK - 1),
+                )
+
+        def open_bank(b, s, tag):
+            bank = psum.tile([P, PACK, SLICE], F32, name="a_bank", tag=tag)
+            chamber_pass(bank, b, s, 0)
+            return bank
+
+        z_rounded, z_mx = {}, {}
+
+        def subtract(bank, b, s):
+            chamber_pass(bank, b, s, 1)
+            if s % 2 == 0:
+                z_rounded[b, s // 2] = held.tile([P, QUARTER * PACK], BF16, name="z_%d_%d" % (b, s // 2), align_bytes=64)
+            width = SLICE * PACK
+            nc.vector.tensor_tensor(
+                out=z_rounded[b, s // 2][:, width * (s % 2) : width * (s % 2 + 1)].rearrange("p (n t) -> p n t", t=PACK),
+                in0=bank[:].rearrange("p t n -> p n t"),
+                in1=size[b, s // 4][:, width * (s % 4) : width * (s % 4 + 1)].rearrange("p (n t) -> p n t", t=PACK),
+                op=SUB,
+            )
+
+        def quantise_z(b, q):
+            codes = held.tile([P, QUARTER], U32, name="z_codes_%d_%d" % (b, q), align_bytes=64)
+            plane = held.tile([P, QUARTER], U8, name="z_plane_%d_%d" % (b, q), align_bytes=64)
+            nc.vector.quantize_mx(out=codes[:].bitcast(FP8X4), scales=plane[:], in_=z_rounded[b, q][:])
+            z_mx[b, q] = codes, plane
+
+        out_rows = out.rearrange("(p u) j -> p u j", u=PACK)
+
+        def planner(q):
+            banks = [psum.tile([P, 2, QUARTER], F32, name="y_bank_%d" % pair, tag="b") for pair in range(2)]
+            for b in range(2):
+                for u in range(PACK):
+                    nc.tensor.matmul_mx(
+                        out=banks[u // 2][:, u % 2, :],
+                        lhsT=w3_mx[b][0][:, P * u : P * (u + 1)].bitcast(FP8X4),
+                        lhsT_scale=w3_mx[b][1][:, P * u : P * (u + 1)],
+                        rhs=z_mx[b, q][0][:].bitcast(FP8X4),
+                        rhs_scale=z_mx[b, q][1][:],
+                        start=(b == 0 and u % 2 == 0),
+                        stop=(b == 1 and u % 2 == 1),
+                    )
+            for pair in range(2):
+                result = held.tile([P, 2, QUARTER], F32, name="result_%d_%d" % (q, pair))
+                for i in range(2):
+                    u = 2 * pair + i
+                    if q == 3 and pair == 1:
+                        nc.vector.tensor_scalar(
+                            out=result[:, i, :], in0=banks[pair][:, i, :], scalar1=gains[:, u : u + 1], scalar2=None, op0=MULT
+                        )
+                    else:
+                        nc.scalar.activation(out=result[:, i, :], in_=banks[pair][:, i, :], func=COPY, scale=gains[:, u : u + 1])
+                nc.sync.dma_start(out=out_rows[:, 2 * pair : 2 * pair + 2, QUARTER * q : QUARTER * (q + 1)], in_=result[:])
+
+        banks = [open_bank(0, s, "ab"[s // 4]) for s in range(8)]
+        for s in range(8):
+            subtract(banks[s], 0, s)
+            if s % 2 == 0 and s > 0:
+                quantise_z(0, s // 2 - 1)
+        banks = [open_bank(1, s, "a") for s in range(4)]
+        for s in range(8):
+            subtract(banks[s], 1, s)
+            if s == 0:
+                quantise_z(0, 3)
+            if s < 4:
+                banks.append(open_bank(1, s + 4, "a"))
+            if s % 2 == 0 and s > 0:
+                quantise_z(1, s // 2 - 1)
+                planner(s // 2 - 1)
+        quantise_z(1, 3)
+        planner(3)

@@ -33,9 +33,8 @@ def tile_list_lock_flight_features_kernel(
     nc = tc.nc
     with ExitStack() as ctx:
         held = ctx.enter_context(tc.tile_pool(name="held", bufs=1))
-        stage = ctx.enter_context(tc.tile_pool(name="stage", bufs=8))
         rounded = ctx.enter_context(tc.tile_pool(name="rounded", bufs=3))
-        psum = ctx.enter_context(tc.psum_pool(name="psum", bufs=4))
+        psum = ctx.enter_context(tc.psum_pool(name="psum", bufs=1))
 
         offsets = held.tile([P, S // 16], U16, name="offsets")
         w2_raw = held.tile([P, 2 * H], U8, name="w2_raw", align_bytes=64)
@@ -45,51 +44,55 @@ def tile_list_lock_flight_features_kernel(
         tab_plane = held.tile([P, T], U8, name="tab_plane", align_bytes=64)
         gains = held.tile([P, PACK], F32, name="gains")
 
-        nc.vector.memset(w2_raw_scales[:].bitcast(I32), 0)
-        nc.vector.memset(xs_plane[:].bitcast(I32), 0)
-        nc.vector.memset(tab_plane[:].bitcast(I32), 0)
+        for zeroed in (w2_raw_scales, xs_plane, tab_plane):
+            nc.vector.memset(zeroed[:].bitcast(I32), 0)
 
-        nc.sync.dma_start(out=w2_raw[:].bitcast(I32), in_=w2_words[0].bitcast(I32))
-        nc.sync.dma_start(out=xs_codes[:].bitcast(I32), in_=xs_words[0].rearrange("p c i -> p (c i)").bitcast(I32))
-        for q in range(4):
-            nc.scalar.dma_start(
-                out=w2_raw_scales[32 * q : 32 * q + 4, :].bitcast(I32), in_=w2_scales[0, 4 * q : 4 * q + 4, :].bitcast(I32)
-            )
-        for q in range(4):
-            nc.scalar.dma_start(
-                out=xs_plane[32 * q : 32 * q + 4, :].bitcast(I32), in_=xs_scales[0, 4 * q : 4 * q + 4, :].bitcast(I32)
-            )
-        for q in range(4):
-            nc.scalar.dma_start(
-                out=tab_plane[32 * q : 32 * q + 8, :].bitcast(I32), in_=tab_scales[:, 4 * q : 4 * q + 4, :].bitcast(I32)
-            )
-        nc.scalar.dma_start(out=gains[:], in_=gain.rearrange("(p u) -> p u", u=PACK))
+        def load_scale_rows(plane, scales):
+            for q in range(4):
+                nc.sync.dma_start(
+                    out=plane[32 * q : 32 * q + 4, :].bitcast(I32), in_=scales[0, 4 * q : 4 * q + 4, :].bitcast(I32)
+                )
 
-        def load_rows(src, row0, col0, width, name):
-            raw = stage.tile([P, PACK, width], F32, name=name, tag="raw")
+        def load_rows(src, row0, col0, width, tag):
+            raw = held.tile([P, PACK, width], F32, name="raw", tag=tag)
             nc.sync.dma_start(
                 out=raw[:], in_=src[row0 : row0 + KP, col0 : col0 + width].rearrange("(p j) c -> p j c", j=PACK)
             )
             return raw
 
-        leak_raw = {}
-        for b in range(2):
-            for h in range(2):
-                leak_raw[b, h] = load_rows(leak, KP * b, HALF * h, HALF, "leak_%d_%d" % (b, h))
-        nc.sync.dma_start(offsets[:], offs)
+        def load_table_scales(odd):
+            for q in (odd, odd + 2):
+                for a in range(2):
+                    row = 32 * q + 4 * a
+                    nc.sync.dma_start(
+                        out=tab_plane[row : row + 4, :].bitcast(I32), in_=tab_scales[a, 4 * q : 4 * q + 4, :].bitcast(I32)
+                    )
 
         def load_table(a):
             words = held.tile([P, T], U32, name="table_%d" % a, align_bytes=64)
             nc.sync.dma_start(out=words[:].bitcast(I32), in_=tab_words[a].rearrange("p t i -> p (t i)").bitcast(I32))
             return words
 
-        table = [load_table(0)]
+        nc.sync.dma_start(out=w2_raw[:].bitcast(I32), in_=w2_words[0].bitcast(I32))
+        nc.sync.dma_start(out=xs_codes[:].bitcast(I32), in_=xs_words[0].rearrange("p c i -> p (c i)").bitcast(I32))
+        load_scale_rows(w2_raw_scales, w2_scales)
+        early = {(0, 0): load_rows(leak, 0, 0, HALF, "leak_0_0")}
+        nc.sync.dma_start(offsets[:], offs)
+        load_scale_rows(xs_plane, xs_scales)
+        nc.sync.dma_start(out=gains[:], in_=gain.rearrange("(p u) -> p u", u=PACK))
+        early[0, 1] = load_rows(leak, 0, HALF, HALF, "leak_0_1")
+        load_table_scales(0)
+        early[1, 0] = load_rows(leak, KP, 0, HALF, "leak_1_0")
         w1_raw = {(0, 0): [load_rows(w1, 0, 0, KP, "w1_0_0")]}
-        table.append(load_table(1))
+        load_table_scales(1)
+        table = [load_table(a) for a in range(2)]
         w1_raw[0, 1] = [load_rows(w1, KP, c0, KP // 2, "w1_0_1_%d" % c0) for c0 in (0, KP // 2)]
         for a in range(2):
             w1_raw[1, a] = [load_rows(w1, KP * a, KP, KP, "w1_1_%d" % a)]
-        w3_raw = [[load_rows(w3, KP * b, 0, N, "w3_%d" % b)] for b in range(2)]
+        w3_raw, late = [], {}
+        for b in range(2):
+            w3_raw.append(load_rows(w3, KP * b, 0, N, "leak_0_%d" % b))
+            late[2 + b] = load_rows(leak, KP, QUARTER * (2 + b), QUARTER, "late_%d" % b)
 
         w2_codes, w2_plane = [], []
         for b in range(2):
@@ -106,85 +109,104 @@ def tile_list_lock_flight_features_kernel(
             w2_codes.append(codes)
             w2_plane.append(plane)
 
+        def pick(window, dtype, name):
+            columns = held.tile([P, S], dtype, name=name, align_bytes=64)
+            nc.vector.tensor_copy(columns[:], window[:].indirect(offsets[:]))
+            return columns
+
+        def gauge_pass(dst, b, t, cols):
+            nc.tensor.matmul_mx(
+                out=dst,
+                lhsT=w2_codes[b][:, 2 * P * t : 2 * P * (t + 1)].bitcast(FP4X4),
+                lhsT_scale=w2_plane[b][:, P * t : P * (t + 1)],
+                rhs=xs_codes[:, cols].bitcast(FP8X4),
+                rhs_scale=xs_plane[:, cols],
+                start=True,
+                stop=True,
+            )
+
+        def absolute(dst, src):
+            nc.scalar.activation(
+                out=dst.rearrange("p (n t) -> p n t", t=PACK), in_=src.rearrange("p t n -> p n t"), func=ABS
+            )
+
         size = {}
-        for b in range(2):
-            for h in range(2):
-                shifted = leak_raw[b, h]
-                for t in range(PACK):
-                    bank = psum.tile([P, HALF], F32, name="c_bank", tag="ab"[t % 2])
-                    nc.tensor.matmul_mx(
-                        out=bank[:],
-                        lhsT=w2_codes[b][:, 2 * P * t : 2 * P * (t + 1)].bitcast(FP4X4),
-                        lhsT_scale=w2_plane[b][:, P * t : P * (t + 1)],
-                        rhs=xs_codes[:, HALF * h : HALF * (h + 1)].bitcast(FP8X4),
-                        rhs_scale=xs_plane[:, HALF * h : HALF * (h + 1)],
-                        start=True,
-                        stop=True,
-                    )
-                    nc.vector.tensor_tensor(out=shifted[:, t, :], in0=bank[:], in1=shifted[:, t, :], op=ADD)
-                size[b, h] = held.tile([P, HALF * PACK], F32, name="size_%d_%d" % (b, h))
-                nc.scalar.activation(
-                    out=size[b, h][:].rearrange("p (c i t) -> p c t i", i=4, t=PACK),
-                    in_=shifted[:].rearrange("p t (c i) -> p c t i", i=4),
-                    func=ABS,
-                )
 
-        picked_plane = held.tile([P, S], U8, name="picked_plane", align_bytes=64)
-        nc.vector.tensor_copy(picked_plane[:], tab_plane[:].indirect(offsets[:]))
-        picked = []
-        for a in range(2):
-            words = held.tile([P, S], U32, name="picked_%d" % a, align_bytes=64)
-            nc.vector.tensor_copy(words[:], table[a][:].indirect(offsets[:]))
-            picked.append(words)
+        def gauge_early(b, h, tag):
+            shifted = early[b, h]
+            for t in range(PACK):
+                bank = psum.tile([P, HALF], F32, name="c_bank", tag="bank_%d" % (PACK * h + t))
+                gauge_pass(bank[:], b, t, slice(HALF * h, HALF * (h + 1)))
+                nc.vector.tensor_tensor(out=shifted[:, t, :], in0=bank[:], in1=shifted[:, t, :], op=ADD)
+            whole = held.tile([P, HALF * PACK], F32, name="size", tag=tag)
+            absolute(whole[:], shifted[:])
+            for i in range(4):
+                size[b, 4 * h + i] = whole[:, SLICE * PACK * i : SLICE * PACK * (i + 1)]
 
-        def quantise_weight(raws, copies, name):
-            grouped = rounded.tile([P, KP * PACK], BF16, name="grouped", align_bytes=64)
+        def gauge_late(s, bank_of):
+            shifted = late[s // 2][:, :, SLICE * (s % 2) : SLICE * (s % 2 + 1)]
+            bank = psum.tile([P, PACK, SLICE], F32, name="c_late", tag="bank_%d" % bank_of)
+            for t in range(PACK):
+                gauge_pass(bank[:, t, :], 1, t, slice(SLICE * s, SLICE * (s + 1)))
+            nc.vector.tensor_tensor(out=shifted, in0=bank[:], in1=shifted, op=ADD)
+            part = held.tile([P, SLICE * PACK], F32, name="size_late_%d" % s)
+            absolute(part[:], shifted)
+            size[1, s] = part[:]
+
+        def quantise_weight(raws, copies, grouped, name, tag):
             dealt = grouped[:].rearrange("p (t m j) -> p m j t", t=PACK, j=PACK)
             step = P // len(raws)
             for i, (raw, copy) in enumerate(zip(raws, copies)):
-                copy(out=dealt[:, step * i : step * (i + 1)], in_=raw[:].rearrange("p j (m t) -> p m j t", t=PACK))
-            codes = held.tile([P, KP], U32, name=name + "_codes", align_bytes=64)
+                copy(out=dealt[:, step * i : step * (i + 1)], in_=raw.rearrange("p j (m t) -> p m j t", t=PACK))
+            codes = held.tile([P, KP], U32, name="codes", tag=tag, align_bytes=64)
             plane = held.tile([P, KP], U8, name=name + "_plane", align_bytes=64)
             nc.vector.quantize_mx(out=codes[:].bitcast(FP8X4), scales=plane[:], in_=grouped[:])
             return codes, plane
 
-        w1_mx = {}
-        for b in range(2):
-            for a in range(2):
-                copies = [nc.scalar.copy, nc.vector.tensor_copy] if len(w1_raw[b, a]) == 2 else [nc.scalar.copy]
-                w1_mx[b, a] = quantise_weight(w1_raw[b, a], copies, "w1_%d_%d" % (b, a))
-        w3_mx = [quantise_weight(w3_raw[b], [nc.scalar.copy], "w3_%d" % b) for b in range(2)]
+        both = (nc.scalar.copy, nc.vector.tensor_copy)
 
-        def chamber_pass(bank, b, s, a):
-            codes, plane = w1_mx[b, a]
-            cols = slice(SLICE * s, SLICE * (s + 1))
-            for t in range(PACK):
-                nc.tensor.matmul_mx(
-                    out=bank[:, t, :],
-                    lhsT=codes[:, P * t : P * (t + 1)].bitcast(FP8X4),
-                    lhsT_scale=plane[:, P * t : P * (t + 1)],
-                    rhs=picked[a][:, cols].bitcast(FP8X4),
-                    rhs_scale=picked_plane[4 * a : P, cols],
-                    start=(a == 0 and t == 0),
-                    stop=(a == 1 and t == PACK - 1),
-                )
+        def quantise_w1(b, a):
+            grouped = rounded.tile([P, KP * PACK], BF16, name="grouped", align_bytes=64)
+            return quantise_weight([raw[:] for raw in w1_raw[b, a]], both, grouped, "w1_%d_%d" % (b, a), "w1_codes_%d_%d" % (b, a))
 
-        def open_bank(b, s, tag):
-            bank = psum.tile([P, PACK, SLICE], F32, name="a_bank", tag=tag)
-            chamber_pass(bank, b, s, 0)
-            return bank
+        def quantise_w3(b):
+            grouped = rounded.tile([P, KP * PACK], BF16, name="grouped", align_bytes=64)
+            return quantise_weight([w3_raw[b][:]], both, grouped, "w3_%d" % b, ("z_0_3", "z_1_0")[b])
+
+        gauge_early(0, 0, "size_0_0")
+        gauge_early(0, 1, "size_0_1")
+        w1_mx = {(0, 0): quantise_w1(0, 0)}
+        gauge_early(1, 0, "w1_0_0")
+        picked_plane = pick(tab_plane, U8, "picked_plane")
+        picked = [pick(table[a], U32, "picked_%d" % a) for a in range(2)]
+        w1_mx[0, 1] = quantise_w1(0, 1)
 
         z_rounded, z_mx = {}, {}
 
-        def subtract(bank, b, s):
-            chamber_pass(bank, b, s, 1)
+        def subtract(b, s):
+            bank = psum.tile([P, PACK, SLICE], F32, name="a_bank", tag="bank_%d" % s)
+            cols = slice(SLICE * s, SLICE * (s + 1))
+            for a in range(2):
+                codes, plane = w1_mx[b, a]
+                for t in range(PACK):
+                    nc.tensor.matmul_mx(
+                        out=bank[:, t, :],
+                        lhsT=codes[:, P * t : P * (t + 1)].bitcast(FP8X4),
+                        lhsT_scale=plane[:, P * t : P * (t + 1)],
+                        rhs=picked[a][:, cols].bitcast(FP8X4),
+                        rhs_scale=picked_plane[4 * a : P, cols],
+                        start=(a == 0 and t == 0),
+                        stop=(a == 1 and t == PACK - 1),
+                    )
             if s % 2 == 0:
-                z_rounded[b, s // 2] = held.tile([P, QUARTER * PACK], BF16, name="z_%d_%d" % (b, s // 2), align_bytes=64)
+                z_rounded[b, s // 2] = held.tile(
+                    [P, QUARTER * PACK], BF16, name="z", tag="z_%d_%d" % (b, s // 2), align_bytes=64
+                )
             width = SLICE * PACK
             nc.vector.tensor_tensor(
                 out=z_rounded[b, s // 2][:, width * (s % 2) : width * (s % 2 + 1)].rearrange("p (n t) -> p n t", t=PACK),
                 in0=bank[:].rearrange("p t n -> p n t"),
-                in1=size[b, s // 4][:, width * (s % 4) : width * (s % 4 + 1)].rearrange("p (n t) -> p n t", t=PACK),
+                in1=size[b, s].rearrange("p (n t) -> p n t", t=PACK),
                 op=SUB,
             )
 
@@ -196,8 +218,8 @@ def tile_list_lock_flight_features_kernel(
 
         out_rows = out.rearrange("(p u) j -> p u j", u=PACK)
 
-        def planner(q):
-            banks = [psum.tile([P, 2, QUARTER], F32, name="y_bank_%d" % pair, tag="b") for pair in range(2)]
+        def planner(q, first_bank):
+            banks = [psum.tile([P, 2, QUARTER], F32, name="y_bank_%d" % pair, tag="bank_%d" % (first_bank + pair)) for pair in range(2)]
             for b in range(2):
                 for u in range(PACK):
                     nc.tensor.matmul_mx(
@@ -221,20 +243,31 @@ def tile_list_lock_flight_features_kernel(
                         nc.scalar.activation(out=result[:, i, :], in_=banks[pair][:, i, :], func=COPY, scale=gains[:, u : u + 1])
                 nc.sync.dma_start(out=out_rows[:, 2 * pair : 2 * pair + 2, QUARTER * q : QUARTER * (q + 1)], in_=result[:])
 
-        banks = [open_bank(0, s, "ab"[s // 4]) for s in range(8)]
         for s in range(8):
-            subtract(banks[s], 0, s)
+            subtract(0, s)
             if s % 2 == 0 and s > 0:
                 quantise_z(0, s // 2 - 1)
-        banks = [open_bank(1, s, "a") for s in range(4)]
-        for s in range(8):
-            subtract(banks[s], 1, s)
+        for a in range(2):
+            w1_mx[1, a] = quantise_w1(1, a)
+        for s in (4, 5):
+            gauge_late(s, s)
+        for s in range(4):
+            subtract(1, s)
             if s == 0:
                 quantise_z(0, 3)
-            if s < 4:
-                banks.append(open_bank(1, s + 4, "a"))
-            if s % 2 == 0 and s > 0:
-                quantise_z(1, s // 2 - 1)
-                planner(s // 2 - 1)
+            if s == 2:
+                quantise_z(1, 0)
+        w3_mx = [quantise_w3(b) for b in range(2)]
+        for s in (6, 7):
+            gauge_late(s, s - 4)
+        subtract(1, 4)
+        quantise_z(1, 1)
+        planner(0, 2)
+        planner(1, 0)
+        subtract(1, 5)
+        subtract(1, 6)
+        quantise_z(1, 2)
+        planner(2, 4)
+        subtract(1, 7)
         quantise_z(1, 3)
-        planner(3)
+        planner(3, 6)

from contextlib import ExitStack

import concourse.mybir as mybir

K, K2, T, S, H, N = 1024, 512, 4096, 1024, 1024, 512
FLOPS = 2 * (K * H * S + K2 * H * S + H * N * S)

F32 = mybir.dt.float32
BF16 = mybir.dt.bfloat16
I32 = mybir.dt.int32
U32 = mybir.dt.uint32
U16 = mybir.dt.uint16
U8 = mybir.dt.uint8
FP8X4 = mybir.dt.float8_e4m3fn_x4
FP4X4 = mybir.dt.float4_e2m1fn_x4
ADD = mybir.AluOpType.add
SUB = mybir.AluOpType.subtract
MULT = mybir.AluOpType.mult
ABS = mybir.ActivationFunctionType.Abs
COPY = mybir.ActivationFunctionType.Copy

P = 128
PACK = 4
KP = P * PACK
HALF = 512
QUARTER = 256
SLICE = 128


def tile_list_lock_flight_features_kernel(
    tc, tab_words, tab_scales, offs, xs_words, xs_scales, w1, w2_words, w2_scales, leak, w3, gain, out
):
    nc = tc.nc
    with ExitStack() as ctx:
        held = ctx.enter_context(tc.tile_pool(name="held", bufs=1))
        rounded = ctx.enter_context(tc.tile_pool(name="rounded", bufs=3))
        psum = ctx.enter_context(tc.psum_pool(name="psum", bufs=1))

        offsets = held.tile([P, S // 16], U16, name="offsets")
        w2_raw = held.tile([P, 2 * H], U8, name="w2_raw", align_bytes=64)
        w2_raw_scales = held.tile([P, H], U8, name="w2_raw_scales", align_bytes=64)
        xs_codes = held.tile([P, S], U32, name="xs_codes", align_bytes=64)
        xs_plane = held.tile([P, S], U8, name="xs_plane", align_bytes=64)
        tab_plane = held.tile([P, T], U8, name="tab_plane", align_bytes=64)
        gains = held.tile([P, PACK], F32, name="gains")

        for zeroed in (w2_raw_scales, xs_plane, tab_plane):
            nc.vector.memset(zeroed[:].bitcast(I32), 0)

        def load_scale_rows(plane, scales):
            for q in range(4):
                nc.sync.dma_start(
                    out=plane[32 * q : 32 * q + 4, :].bitcast(I32), in_=scales[0, 4 * q : 4 * q + 4, :].bitcast(I32)
                )

        def load_rows(src, row0, col0, width, tag):
            raw = held.tile([P, PACK, width], F32, name="raw", tag=tag)
            nc.sync.dma_start(
                out=raw[:], in_=src[row0 : row0 + KP, col0 : col0 + width].rearrange("(p j) c -> p j c", j=PACK)
            )
            return raw

        def load_table_scales(odd):
            for q in (odd, odd + 2):
                for a in range(2):
                    row = 32 * q + 4 * a
                    nc.sync.dma_start(
                        out=tab_plane[row : row + 4, :].bitcast(I32), in_=tab_scales[a, 4 * q : 4 * q + 4, :].bitcast(I32)
                    )

        def load_table(a):
            words = held.tile([P, T], U32, name="table_%d" % a, align_bytes=64)
            nc.sync.dma_start(out=words[:].bitcast(I32), in_=tab_words[a].rearrange("p t i -> p (t i)").bitcast(I32))
            return words

        nc.sync.dma_start(out=w2_raw[:].bitcast(I32), in_=w2_words[0].bitcast(I32))
        nc.sync.dma_start(out=xs_codes[:].bitcast(I32), in_=xs_words[0].rearrange("p c i -> p (c i)").bitcast(I32))
        load_scale_rows(w2_raw_scales, w2_scales)
        early = {(0, 0): load_rows(leak, 0, 0, HALF, "leak_0_0")}
        nc.sync.dma_start(offsets[:], offs)
        load_scale_rows(xs_plane, xs_scales)
        nc.sync.dma_start(out=gains[:], in_=gain.rearrange("(p u) -> p u", u=PACK))
        early[0, 1] = load_rows(leak, 0, HALF, HALF, "leak_0_1")
        load_table_scales(0)
        early[1, 0] = load_rows(leak, KP, 0, HALF, "leak_1_0")
        w1_raw = {(0, 0): [load_rows(w1, 0, 0, KP, "w1_0_0")]}
        load_table_scales(1)
        table = [load_table(a) for a in range(2)]
        w1_raw[0, 1] = [load_rows(w1, KP, c0, KP // 2, "w1_0_1_%d" % c0) for c0 in (0, KP // 2)]
        for a in range(2):
            w1_raw[1, a] = [load_rows(w1, KP * a, KP, KP, "w1_1_%d" % a)]
        w3_raw, late = [], {}
        for b in range(2):
            w3_raw.append(load_rows(w3, KP * b, 0, N, "leak_0_%d" % b))
            late[2 + b] = load_rows(leak, KP, QUARTER * (2 + b), QUARTER, "late_%d" % b)

        w2_codes, w2_plane = [], []
        for b in range(2):
            codes = held.tile([P, 2 * KP], U8, name="w2_codes_%d" % b, align_bytes=64)
            plane = held.tile([P, KP], U8, name="w2_plane_%d" % b, align_bytes=64)
            nc.vector.tensor_copy(
                out=codes[:].rearrange("p (t m e) -> p t m e", t=PACK, e=2),
                in_=w2_raw[:, 2 * KP * b : 2 * KP * (b + 1)].rearrange("p (m t e) -> p t m e", t=PACK, e=2),
            )
            nc.vector.tensor_copy(
                out=plane[:].rearrange("p (t m) -> p t m", t=PACK),
                in_=w2_raw_scales[:, KP * b : KP * (b + 1)].rearrange("p (m t) -> p t m", t=PACK),
            )
            w2_codes.append(codes)
            w2_plane.append(plane)

        def pick(window, dtype, name):
            columns = held.tile([P, S], dtype, name=name, align_bytes=64)
            nc.vector.tensor_copy(columns[:], window[:].indirect(offsets[:]))
            return columns

        def gauge_pass(dst, b, t, cols):
            nc.tensor.matmul_mx(
                out=dst,
                lhsT=w2_codes[b][:, 2 * P * t : 2 * P * (t + 1)].bitcast(FP4X4),
                lhsT_scale=w2_plane[b][:, P * t : P * (t + 1)],
                rhs=xs_codes[:, cols].bitcast(FP8X4),
                rhs_scale=xs_plane[:, cols],
                start=True,
                stop=True,
            )

        def absolute(dst, src):
            nc.scalar.activation(
                out=dst.rearrange("p (n t) -> p n t", t=PACK), in_=src.rearrange("p t n -> p n t"), func=ABS
            )

        size = {}

        def gauge_early(b, h, tag):
            shifted = early[b, h]
            for t in range(PACK):
                bank = psum.tile([P, HALF], F32, name="c_bank", tag="bank_%d" % (PACK * h + t))
                gauge_pass(bank[:], b, t, slice(HALF * h, HALF * (h + 1)))
                nc.vector.tensor_tensor(out=shifted[:, t, :], in0=bank[:], in1=shifted[:, t, :], op=ADD)
            whole = held.tile([P, HALF * PACK], F32, name="size", tag=tag)
            absolute(whole[:], shifted[:])
            for i in range(4):
                size[b, 4 * h + i] = whole[:, SLICE * PACK * i : SLICE * PACK * (i + 1)]

        def gauge_late(s, bank_of):
            shifted = late[s // 2][:, :, SLICE * (s % 2) : SLICE * (s % 2 + 1)]
            bank = psum.tile([P, PACK, SLICE], F32, name="c_late", tag="bank_%d" % bank_of)
            for t in range(PACK):
                gauge_pass(bank[:, t, :], 1, t, slice(SLICE * s, SLICE * (s + 1)))
            nc.vector.tensor_tensor(out=shifted, in0=bank[:], in1=shifted, op=ADD)
            part = held.tile([P, SLICE * PACK], F32, name="size_late_%d" % s)
            absolute(part[:], shifted)
            size[1, s] = part[:]

        def quantise_weight(raws, copies, grouped, name, tag):
            dealt = grouped[:].rearrange("p (t m j) -> p m j t", t=PACK, j=PACK)
            step = P // len(raws)
            for i, (raw, copy) in enumerate(zip(raws, copies)):
                copy(out=dealt[:, step * i : step * (i + 1)], in_=raw.rearrange("p j (m t) -> p m j t", t=PACK))
            codes = held.tile([P, KP], U32, name="codes", tag=tag, align_bytes=64)
            plane = held.tile([P, KP], U8, name=name + "_plane", align_bytes=64)
            nc.vector.quantize_mx(out=codes[:].bitcast(FP8X4), scales=plane[:], in_=grouped[:])
            return codes, plane

        both = (nc.scalar.copy, nc.vector.tensor_copy)

        def quantise_w1(b, a):
            grouped = rounded.tile([P, KP * PACK], BF16, name="grouped", align_bytes=64)
            return quantise_weight([raw[:] for raw in w1_raw[b, a]], both, grouped, "w1_%d_%d" % (b, a), "w1_codes_%d_%d" % (b, a))

        def quantise_w3(b):
            grouped = rounded.tile([P, KP * PACK], BF16, name="grouped", align_bytes=64)
            return quantise_weight([w3_raw[b][:]], both, grouped, "w3_%d" % b, ("z_0_3", "z_1_0")[b])

        gauge_early(0, 0, "size_0_0")
        gauge_early(0, 1, "size_0_1")
        w1_mx = {(0, 0): quantise_w1(0, 0)}
        gauge_early(1, 0, "w1_0_0")
        picked_plane = pick(tab_plane, U8, "picked_plane")
        picked = [pick(table[a], U32, "picked_%d" % a) for a in range(2)]
        w1_mx[0, 1] = quantise_w1(0, 1)

        z_rounded, z_mx = {}, {}

        def subtract(b, s):
            bank = psum.tile([P, PACK, SLICE], F32, name="a_bank", tag="bank_%d" % s)
            cols = slice(SLICE * s, SLICE * (s + 1))
            for a in range(2):
                codes, plane = w1_mx[b, a]
                for t in range(PACK):
                    nc.tensor.matmul_mx(
                        out=bank[:, t, :],
                        lhsT=codes[:, P * t : P * (t + 1)].bitcast(FP8X4),
                        lhsT_scale=plane[:, P * t : P * (t + 1)],
                        rhs=picked[a][:, cols].bitcast(FP8X4),
                        rhs_scale=picked_plane[4 * a : P, cols],
                        start=(a == 0 and t == 0),
                        stop=(a == 1 and t == PACK - 1),
                    )
            if s % 2 == 0:
                z_rounded[b, s // 2] = held.tile(
                    [P, QUARTER * PACK], BF16, name="z", tag="z_%d_%d" % (b, s // 2), align_bytes=64
                )
            width = SLICE * PACK
            nc.vector.tensor_tensor(
                out=z_rounded[b, s // 2][:, width * (s % 2) : width * (s % 2 + 1)].rearrange("p (n t) -> p n t", t=PACK),
                in0=bank[:].rearrange("p t n -> p n t"),
                in1=size[b, s].rearrange("p (n t) -> p n t", t=PACK),
                op=SUB,
            )

        def quantise_z(b, q):
            codes = held.tile([P, QUARTER], U32, name="z_codes_%d_%d" % (b, q), align_bytes=64)
            plane = held.tile([P, QUARTER], U8, name="z_plane_%d_%d" % (b, q), align_bytes=64)
            nc.vector.quantize_mx(out=codes[:].bitcast(FP8X4), scales=plane[:], in_=z_rounded[b, q][:])
            z_mx[b, q] = codes, plane

        out_rows = out.rearrange("(p u) j -> p u j", u=PACK)

        def planner(q, first_bank):
            banks = [psum.tile([P, 2, QUARTER], F32, name="y_bank_%d" % pair, tag="bank_%d" % (first_bank + pair)) for pair in range(2)]
            for b in range(2):
                for u in range(PACK):
                    nc.tensor.matmul_mx(
                        out=banks[u // 2][:, u % 2, :],
                        lhsT=w3_mx[b][0][:, P * u : P * (u + 1)].bitcast(FP8X4),
                        lhsT_scale=w3_mx[b][1][:, P * u : P * (u + 1)],
                        rhs=z_mx[b, q][0][:].bitcast(FP8X4),
                        rhs_scale=z_mx[b, q][1][:],
                        start=(b == 0 and u % 2 == 0),
                        stop=(b == 1 and u % 2 == 1),
                    )
            for pair in range(2):
                result = held.tile([P, 2, QUARTER], F32, name="result_%d_%d" % (q, pair))
                for i in range(2):
                    u = 2 * pair + i
                    if q == 3 and pair == 1:
                        nc.vector.tensor_scalar(
                            out=result[:, i, :], in0=banks[pair][:, i, :], scalar1=gains[:, u : u + 1], scalar2=None, op0=MULT
                        )
                    else:
                        nc.scalar.activation(out=result[:, i, :], in_=banks[pair][:, i, :], func=COPY, scale=gains[:, u : u + 1])
                nc.sync.dma_start(out=out_rows[:, 2 * pair : 2 * pair + 2, QUARTER * q : QUARTER * (q + 1)], in_=result[:])

        for s in range(8):
            subtract(0, s)
            if s % 2 == 0 and s > 0:
                quantise_z(0, s // 2 - 1)
        for a in range(2):
            w1_mx[1, a] = quantise_w1(1, a)
        for s in (4, 5):
            gauge_late(s, s)
        for s in range(4):
            subtract(1, s)
            if s == 0:
                quantise_z(0, 3)
            if s == 2:
                quantise_z(1, 0)
        w3_mx = [quantise_w3(b) for b in range(2)]
        for s in (6, 7):
            gauge_late(s, s - 4)
        subtract(1, 4)
        quantise_z(1, 1)
        planner(0, 2)
        planner(1, 0)
        subtract(1, 5)
        subtract(1, 6)
        quantise_z(1, 2)
        planner(2, 4)
        subtract(1, 7)
        quantise_z(1, 3)
        planner(3, 6)
